import numpy as np, ml_dtypes
CORES = [2,10,130,138,258,266,386,394]
N = 8
def setup_inputs(rng):
    return {"x": rng.standard_normal((N, 128, 64), dtype=np.float32).astype(ml_dtypes.bfloat16)}
def reference(x):
    s = x.max(axis=0)
    b = 64 // N
    return {"y": np.stack([s[:, r * b:(r + 1) * b] for r in range(N)])}

@@ -1,0 +1,58 @@
+from concourse.bass import RemoteDMATransfer, DstId
+
+SCRATCH = {
+    "xs": ("sbuf", [128, 64], "bfloat16"),
+    "rc": ("sbuf", [128, 32], "bfloat16"),
+    "col": ("sbuf", [128, 32], "bfloat16"),
+    "out": ("sbuf", [128, 8], "bfloat16"),
+}
+SEMAPHORES = ["ldA", "ldB", "s1", "s2", "s3", "snd", "st"]
+
+CABLE = {0: 3, 3: 0, 1: 2, 2: 1}
+
+
+def rank_program(g, core, T, topo):
+    S = T.sem
+    rank = T.rank_of(core)
+    if rank is None:
+        owner = core - 1
+        if core % 8 != 3 or T.rank_of(owner) is None:
+            return
+        g.wait_ge(S.s2, 16)
+        rid, pid = topo.addr(owner, core)
+        g.remote_dma_fused([RemoteDMATransfer(
+            dst_ids=[DstId(rid=rid, pnc=pid)], dma_engine_mask=0xFFFF, remote_sem=S.s3,
+            srcs=[T.col[:, 8 * i:8 * i + 8] for i in range(4)], dsts=[T.out[:]], alu_op=2)], local_sem=S.snd)
+        g.wait_ge(S.snd, 16)
+        return
+
+    k = rank // 4
+    i = rank % 4
+    own, oth = 32 * k, 32 * (1 - k)
+    g.dma_start(T.xs[:, oth:oth + 32], T.x[:, oth:oth + 32]).then_inc(S.ldA, 16)
+    g.dma_start(T.xs[:, own:own + 32], T.x[:, own:own + 32]).then_inc(S.ldB, 16)
+
+    h = topo.host(core)
+    partner = CABLE[h] * 128 + core % 128
+    rid, pid = topo.addr(partner, core)
+    g.wait_ge(S.ldA, 16)
+    g.remote_dma(T.rc[:], T.xs[:, oth:oth + 32], S.s1, S.snd, pid, rid, 0xFF)
+
+    g.wait_ge(S.ldB, 16)
+    g.wait_ge(S.s1, 8)
+    trs = []
+    for j in range(4):
+        q = T.cores[4 * k + j] + 1
+        rel = i ^ j
+        m = {0: 0xFF00, 1: 0x0030, 2: 0x00C0, 3: 0x000F}[rel]
+        rid, pid = topo.addr(q, core)
+        trs.append(RemoteDMATransfer(
+            dst_ids=[DstId(rid=rid, pnc=pid)], dma_engine_mask=m, remote_sem=S.s2,
+            srcs=[T.xs[:, own + 8 * j:own + 8 * j + 8], T.rc[:, 8 * j:8 * j + 8]],
+            dsts=[T.col[:, 8 * i:8 * i + 8]], alu_op=2))
+    g.remote_dma_fused(trs, local_sem=S.snd)
+
+    g.wait_ge(S.s3, 16)
+    g.dma_start(T.y[:], T.out[:]).then_inc(S.st, 16)
+    g.wait_ge(S.st, 16)
+    g.wait_ge(S.snd, 24)

@@ -1,10 +1,11 @@
 from concourse.bass import RemoteDMATransfer, DstId
 
 SCRATCH = {
-    "xs": ("sbuf", [128, 64], "bfloat16"),
-    "rc": ("sbuf", [128, 32], "bfloat16"),
-    "col": ("sbuf", [128, 32], "bfloat16"),
-    "out": ("sbuf", [128, 8], "bfloat16"),
+    "xa": ("dram", [4, 128, 8], "bfloat16"),
+    "xb": ("dram", [4, 128, 8], "bfloat16"),
+    "rd": ("dram", [4, 128, 8], "bfloat16"),
+    "cd": ("dram", [4, 128, 8], "bfloat16"),
+    "fd": ("dram", [4, 128, 8], "bfloat16"),
 }
 SEMAPHORES = ["ldA", "ldB", "s1", "s2", "s3", "snd", "st"]
 
@@ -15,44 +16,49 @@ def rank_program(g, core, T, topo):
     S = T.sem
     rank = T.rank_of(core)
     if rank is None:
-        owner = core - 1
-        if core % 8 != 3 or T.rank_of(owner) is None:
+        r = T.rank_of(core - 1) if core % 8 == 3 else None
+        if r is None:
             return
+        k, m = r // 4, r % 4
+        ids = []
+        for j in range(4):
+            rid, pid = topo.addr(T.cores[4 * k + j], core)
+            ids.append(DstId(rid=rid, pnc=pid))
         g.wait_ge(S.s2, 16)
-        rid, pid = topo.addr(owner, core)
         g.remote_dma_fused([RemoteDMATransfer(
-            dst_ids=[DstId(rid=rid, pnc=pid)], dma_engine_mask=0xFFFF, remote_sem=S.s3,
-            srcs=[T.col[:, 8 * i:8 * i + 8] for i in range(4)], dsts=[T.out[:]], alu_op=2)], local_sem=S.snd)
-        g.wait_ge(S.snd, 16)
+            dst_ids=ids, dma_engine_mask=0x00FF, remote_sem=S.s3,
+            srcs=[T.cd[i] for i in range(4)], dsts=[T.fd[m] for j in range(4)], alu_op=2)], local_sem=S.snd)
+        g.wait_ge(S.snd, 8)
         return
 
     k = rank // 4
     i = rank % 4
     own, oth = 32 * k, 32 * (1 - k)
-    g.dma_start(T.xs[:, oth:oth + 32], T.x[:, oth:oth + 32]).then_inc(S.ldA, 16)
-    g.dma_start(T.xs[:, own:own + 32], T.x[:, own:own + 32]).then_inc(S.ldB, 16)
+    g.dma_start(T.xa[:], T.x[:, oth:oth + 32]).then_inc(S.ldA, 16)
+    g.dma_start(T.xb[:], T.x[:, own:own + 32]).then_inc(S.ldB, 16)
 
     h = topo.host(core)
     partner = CABLE[h] * 128 + core % 128
     rid, pid = topo.addr(partner, core)
     g.wait_ge(S.ldA, 16)
-    g.remote_dma(T.rc[:], T.xs[:, oth:oth + 32], S.s1, S.snd, pid, rid, 0xFF)
+    g.remote_dma_fused([RemoteDMATransfer(
+        dst_ids=[DstId(rid=rid, pnc=pid)], dma_engine_mask=0x3 << (2 * m), remote_sem=S.s1,
+        src=T.xa[m], dst=T.rd[m]) for m in range(4)], local_sem=S.snd)
 
     g.wait_ge(S.ldB, 16)
     g.wait_ge(S.s1, 8)
     trs = []
-    for j in range(4):
-        q = T.cores[4 * k + j] + 1
-        rel = i ^ j
-        m = {0: 0xFF00, 1: 0x0030, 2: 0x00C0, 3: 0x000F}[rel]
+    for m in range(4):
+        q = T.cores[4 * k + m] + 1
+        rel = i ^ m
+        mask = {0: 0xFF00, 1: 0x0030, 2: 0x00C0, 3: 0x000F}[rel]
         rid, pid = topo.addr(q, core)
         trs.append(RemoteDMATransfer(
-            dst_ids=[DstId(rid=rid, pnc=pid)], dma_engine_mask=m, remote_sem=S.s2,
-            srcs=[T.xs[:, own + 8 * j:own + 8 * j + 8], T.rc[:, 8 * j:8 * j + 8]],
-            dsts=[T.col[:, 8 * i:8 * i + 8]], alu_op=2))
+            dst_ids=[DstId(rid=rid, pnc=pid)], dma_engine_mask=mask, remote_sem=S.s2,
+            srcs=[T.xb[m], T.rd[m]], dsts=[T.cd[i]], alu_op=2))
     g.remote_dma_fused(trs, local_sem=S.snd)
 
-    g.wait_ge(S.s3, 16)
-    g.dma_start(T.y[:], T.out[:]).then_inc(S.st, 16)
+    g.wait_ge(S.s3, 32)
+    g.dma_start(T.y[:], T.fd[:, i::4, :]).then_inc(S.st, 16)
     g.wait_ge(S.st, 16)
     g.wait_ge(S.snd, 24)

from concourse.bass import RemoteDMATransfer, DstId

SCRATCH = {
    "xa": ("dram", [4, 128, 8], "bfloat16"),
    "xb": ("dram", [4, 128, 8], "bfloat16"),
    "rd": ("dram", [4, 128, 8], "bfloat16"),
    "cd": ("dram", [4, 128, 8], "bfloat16"),
    "fd": ("dram", [4, 128, 8], "bfloat16"),
}
SEMAPHORES = ["ldA", "ldB", "s1", "s2", "s3", "snd", "st"]

CABLE = {0: 3, 3: 0, 1: 2, 2: 1}


def rank_program(g, core, T, topo):
    S = T.sem
    rank = T.rank_of(core)
    if rank is None:
        r = T.rank_of(core - 1) if core % 8 == 3 else None
        if r is None:
            return
        k, m = r // 4, r % 4
        ids = []
        for j in range(4):
            rid, pid = topo.addr(T.cores[4 * k + j], core)
            ids.append(DstId(rid=rid, pnc=pid))
        g.wait_ge(S.s2, 16)
        g.remote_dma_fused([RemoteDMATransfer(
            dst_ids=ids, dma_engine_mask=0x00FF, remote_sem=S.s3,
            srcs=[T.cd[i] for i in range(4)], dsts=[T.fd[m] for j in range(4)], alu_op=2)], local_sem=S.snd)
        g.wait_ge(S.snd, 8)
        return

    k = rank // 4
    i = rank % 4
    own, oth = 32 * k, 32 * (1 - k)
    g.dma_start(T.xa[:], T.x[:, oth:oth + 32]).then_inc(S.ldA, 16)
    g.dma_start(T.xb[:], T.x[:, own:own + 32]).then_inc(S.ldB, 16)

    h = topo.host(core)
    partner = CABLE[h] * 128 + core % 128
    rid, pid = topo.addr(partner, core)
    g.wait_ge(S.ldA, 16)
    g.remote_dma_fused([RemoteDMATransfer(
        dst_ids=[DstId(rid=rid, pnc=pid)], dma_engine_mask=0x3 << (2 * m), remote_sem=S.s1,
        src=T.xa[m], dst=T.rd[m]) for m in range(4)], local_sem=S.snd)

    g.wait_ge(S.ldB, 16)
    g.wait_ge(S.s1, 8)
    trs = []
    for m in range(4):
        q = T.cores[4 * k + m] + 1
        rel = i ^ m
        mask = {0: 0xFF00, 1: 0x0030, 2: 0x00C0, 3: 0x000F}[rel]
        rid, pid = topo.addr(q, core)
        trs.append(RemoteDMATransfer(
            dst_ids=[DstId(rid=rid, pnc=pid)], dma_engine_mask=mask, remote_sem=S.s2,
            srcs=[T.xb[m], T.rd[m]], dsts=[T.cd[i]], alu_op=2))
    g.remote_dma_fused(trs, local_sem=S.snd)

    g.wait_ge(S.s3, 32)
    g.dma_start(T.y[:], T.fd[:, i::4, :]).then_inc(S.st, 16)
    g.wait_ge(S.st, 16)
    g.wait_ge(S.snd, 24)
